import numpy as np
import ml_dtypes


def mxq(x, axis, fmt="e4m3"):
    dtype, down = {"e4m3": (ml_dtypes.float8_e4m3fn, 7), "e5m2": (ml_dtypes.float8_e5m2, 14)}[fmt]
    v = np.moveaxis(np.asarray(x, np.float32).astype(ml_dtypes.bfloat16).astype(np.float64), axis, -1)
    blocks = v.reshape(v.shape[:-1] + (-1, 32))
    amax = np.abs(blocks).max(-1, keepdims=True)
    byte = np.maximum(np.where(amax > 0, np.frexp(amax)[1] - 1 + 127, 0) - down, 1)
    scale = np.exp2(byte - 127.0)
    codes = (blocks / scale).astype(np.float32).astype(dtype).astype(np.float64)
    return np.moveaxis((codes * scale).reshape(v.shape), -1, axis)


WIDE = False


def mx_kscale(k):
    if not WIDE:
        return np.ones(k)
    levels = np.array([10, -10, 5, -5, 0])
    if k % 512:
        return np.exp2(np.random.permutation(np.resize(levels, k // 32))).repeat(32)
    a = np.empty((k // 512, 16))
    for p in range(k // 512):
        a[p, :8] = np.random.permutation(np.resize(levels, 8))
        for g in range(8):
            far = levels[np.abs(levels - a[p, g]) >= 10]
            a[p, g + 8] = far[np.random.randint(len(far))]
    return np.exp2(a.ravel()).repeat(32)


def f64(x):
    return np.asarray(x).astype(np.float64)


E2M1 = np.array([0.0, 0.5, 1.0, 1.5, 2.0, 3.0, 4.0, 6.0, -0.0, -0.5, -1.0, -1.5, -2.0, -3.0, -4.0, -6.0])


def pack_weight(w, fmt):
    k, n = w.shape
    w = f64(np.asarray(w, np.float32).astype(ml_dtypes.bfloat16)).reshape(k // 32, 32, n)
    amax = np.abs(w).max(1)
    if fmt == "e4m3":
        byte = np.frexp(amax)[1] - 1 + 127 - 7
    else:
        mant, ex = np.frexp(amax / 6.0)
        byte = np.where(mant > 0.5, ex, ex - 1) + 127
    byte = np.clip(np.where(amax > 0, byte, 1), 1, 254)
    scaled = (w * np.exp2(127.0 - byte)[:, None, :]).reshape(k, n).astype(np.float32)
    by_word = np.ascontiguousarray(scaled.reshape(k // 512, 128, 4, n).transpose(0, 1, 3, 2))
    if fmt == "e4m3":
        words = by_word.astype(ml_dtypes.float8_e4m3fn).view(np.uint8)
    else:
        c = by_word.astype(ml_dtypes.float4_e2m1fn).view(np.uint8) & 0xF
        words = (c[..., 0::2] | (c[..., 1::2] << 4)).reshape(k // 512, 128, 2 * n)
    return np.ascontiguousarray(words), np.ascontiguousarray(byte.astype(np.uint8).reshape(k // 512, 16, n))


def unpack_weight(words, scales, fmt):
    g, _, n = scales.shape
    words = np.ascontiguousarray(words).reshape(g, 128, n, -1)
    if fmt == "e4m3":
        vals = words.view(ml_dtypes.float8_e4m3fn).astype(np.float64)
    else:
        nib = np.empty((g, 128, n, 4), np.uint8)
        nib[..., 0::2] = words & 0xF
        nib[..., 1::2] = words >> 4
        vals = E2M1[nib]
    vals = vals * np.repeat(np.exp2(scales.astype(np.float64) - 127.0), 8, axis=1)[..., None]
    return vals.transpose(0, 1, 3, 2).reshape(g * 512, n)


K, M, T = 1024, 512, 1536


def setup_inputs():
    n = np.random.standard_normal
    s = mx_kscale(K)[:, None]
    x = n((K, T)) * s
    x4 = pack_weight(x, "e2m1")
    rest = x - unpack_weight(*x4, "e2m1")
    p_w4 = pack_weight(n((K, M)) / np.sqrt(K) / s, "e2m1")
    return {
        "x4_words": x4[0],
        "x4_scales": x4[1],
        "xr": (rest).astype(np.float32),
        "w4_words": p_w4[0],
        "w4_scales": p_w4[1],
    }


def reference(x4_words, x4_scales, xr, w4_words, w4_scales):
    x4_ = unpack_weight(x4_words, x4_scales, "e2m1")
    xr_ = mxq(f64(xr), 0, "e4m3")
    w4_ = unpack_weight(w4_words, w4_scales, "e2m1")
    y = x4_.T @ w4_ + xr_.T @ w4_
    return y

@@ -1,0 +1,156 @@
+from contextlib import ExitStack
+
+import concourse.mybir as mybir
+
+K, N, T = 1024, 512, 1536
+FLOPS = 2 * 2 * K * N * T
+
+F32 = mybir.dt.float32
+BF16 = mybir.dt.bfloat16
+I32 = mybir.dt.int32
+U32 = mybir.dt.uint32
+U8 = mybir.dt.uint8
+E4M3X4 = mybir.dt.float8_e4m3fn_x4
+E2M1X4 = mybir.dt.float4_e2m1fn_x4
+
+P = 128
+PACK = 4
+K_PASS = P * PACK
+PASSES = K // K_PASS
+CHUNK = 768
+GROUP = 256
+TILES = T // P
+BANKS = 8
+
+
+def tile_mix_xres_tm_none_kernel(tc, x4_words, x4_scales, xr, w4_words, w4_scales, out):
+    nc = tc.nc
+    with ExitStack() as ctx:
+        keep = ctx.enter_context(tc.tile_pool(name="keep", bufs=1))
+        psum = ctx.enter_context(tc.psum_pool(name="psum", bufs=1))
+
+        w_words = keep.tile([P, PASSES * 2 * N], U8, name="w_words", align_bytes=64)
+        x_words = keep.tile([P, PASSES * 2 * T], U8, name="x_words", align_bytes=64)
+        w_scales = keep.tile([P, PASSES * N], U8, name="w_scales", align_bytes=64)
+        x_scales = keep.tile([P, PASSES * T], U8, name="x_scales", align_bytes=64)
+
+        ctx.enter_context(tc.manual_schedule())
+
+        nc.vector.memset(x_scales[:].bitcast(I32), 0)
+        nc.gpsimd.memset(w_scales[:].bitcast(I32), 0)
+
+        nc.sync.dma_start(
+            out=w_words[:].rearrange("p (a n) -> p a n", a=PASSES).bitcast(I32),
+            in_=w4_words.rearrange("a p n -> p a n").bitcast(I32),
+        )
+        nc.sync.dma_start(
+            out=x_words[:].rearrange("p (a n) -> p a n", a=PASSES).bitcast(I32),
+            in_=x4_words.rearrange("a p n -> p a n").bitcast(I32),
+        )
+        for r in range(4):
+            nc.gpsimd.dma_start(
+                out=w_scales[r:P:32, :].rearrange("q (a n) -> q a n", a=PASSES).bitcast(I32),
+                in_=w4_scales.rearrange("a (q r) n -> r q a n", r=4)[r].bitcast(I32),
+            )
+            nc.scalar.dma_start(
+                out=x_scales[r:P:32, :].rearrange("q (a t) -> q a t", a=PASSES).bitcast(I32),
+                in_=x4_scales.rearrange("a (q r) t -> r q a t", r=4)[r].bitcast(I32),
+            )
+        raw = {}
+        for a in range(PASSES):
+            for c in range(T // CHUNK):
+                raw[a, c] = keep.tile([P, PACK, CHUNK], F32, name=f"raw{a}{c}")
+                nc.sync.dma_start(
+                    out=raw[a, c][:],
+                    in_=xr[a * K_PASS : (a + 1) * K_PASS, c * CHUNK : (c + 1) * CHUNK].rearrange("(p j) t -> p j t", j=PACK),
+                )
+
+        grouped, codes, scales, acc = {}, {}, {}, {}
+
+        def cast(copy, a, g):
+            grouped[a, g] = keep.tile([P, GROUP, PACK], BF16, name=f"grouped{a}{g}", align_bytes=64)
+            c, first = divmod(g * GROUP, CHUNK)
+            copy(
+                out=grouped[a, g][:].rearrange("p (b i) j -> p b j i", i=4),
+                in_=raw[a, c][:, :, first : first + GROUP].rearrange("p j (b i) -> p b j i", i=4),
+            )
+
+        def quantize(a, g):
+            codes[a, g] = keep.tile([P, GROUP], U32, name=f"codes{a}{g}", align_bytes=64)
+            scales[a, g] = keep.tile([P, GROUP], U8, name=f"scales{a}{g}", align_bytes=64)
+            nc.vector.quantize_mx(
+                out=codes[a, g][:].bitcast(E4M3X4),
+                scales=scales[a, g][:],
+                in_=grouped[a, g][:].rearrange("p t j -> p (t j)"),
+            )
+
+        def multiply(i, a, lhs, lhs_scale, start, stop):
+            nc.tensor.matmul_mx(
+                out=acc[i][:],
+                lhsT=lhs,
+                lhsT_scale=lhs_scale,
+                rhs=w_words[:, a * 2 * N : (a + 1) * 2 * N].bitcast(E2M1X4),
+                rhs_scale=w_scales[:, a * N : (a + 1) * N],
+                start=start,
+                stop=stop,
+            )
+
+        def multiply_x4(i):
+            acc[i] = psum.tile([P, N], F32, name=f"acc{i % BANKS}")
+            for a in range(PASSES):
+                col = a * T + i * P
+                multiply(i, a, x_words[:, 2 * col : 2 * (col + P)].bitcast(E2M1X4), x_scales[:, col : col + P], a == 0, False)
+
+        def multiply_xr(a, g):
+            for h in range(GROUP // P):
+                cols = slice(h * P, (h + 1) * P)
+                multiply(g * (GROUP // P) + h, a, codes[a, g][:, cols].bitcast(E4M3X4), scales[a, g][:, cols], False, a == PASSES - 1)
+
+        def finish(copy, i):
+            result = keep.tile([P, N], F32, name=f"result{i}")
+            copy(out=result[:], in_=acc[i][:])
+            nc.sync.dma_start(out=out[i * P : (i + 1) * P, :], in_=result[:])
+
+        vec, act = nc.vector.tensor_copy, nc.scalar.copy
+
+        for i in range(BANKS):
+            multiply_x4(i)
+        for first in (0, 3):
+            cast(act, 0, first + 2)
+            cast(vec, 0, first)
+            cast(vec, 0, first + 1)
+            for g in range(first, first + 3):
+                quantize(0, g)
+                if g < BANKS // 2:
+                    multiply_xr(0, g)
+
+        cast(act, 1, 2)
+        cast(vec, 1, 0)
+        cast(vec, 1, 1)
+        for g in range(3):
+            quantize(1, g)
+        multiply_xr(1, 0)
+        finish(act, 0)
+        finish(vec, 1)
+        multiply_xr(1, 1)
+        finish(act, 2)
+        finish(vec, 3)
+        for i in (8, 9):
+            multiply_x4(i)
+        multiply_xr(0, 4)
+        multiply_xr(1, 2)
+        finish(act, 4)
+        finish(act, 5)
+        for i in (10, 11):
+            multiply_x4(i)
+        multiply_xr(0, 5)
+
+        cast(act, 1, 5)
+        cast(vec, 1, 3)
+        cast(vec, 1, 4)
+        for g in range(3, 6):
+            quantize(1, g)
+        for g in range(3, 6):
+            multiply_xr(1, g)
+            finish(act, 2 * g)
+            finish(vec, 2 * g + 1)

@@ -36,34 +36,41 @@ def tile_mix_xres_tm_none_kernel(tc, x4_words, x4_scales, xr, w4_words, w4_scale
 
         ctx.enter_context(tc.manual_schedule())
 
-        nc.vector.memset(x_scales[:].bitcast(I32), 0)
         nc.gpsimd.memset(w_scales[:].bitcast(I32), 0)
+        nc.vector.memset(x_scales[:].bitcast(I32), 0)
 
-        nc.sync.dma_start(
-            out=w_words[:].rearrange("p (a n) -> p a n", a=PASSES).bitcast(I32),
-            in_=w4_words.rearrange("a p n -> p a n").bitcast(I32),
-        )
-        nc.sync.dma_start(
-            out=x_words[:].rearrange("p (a n) -> p a n", a=PASSES).bitcast(I32),
-            in_=x4_words.rearrange("a p n -> p a n").bitcast(I32),
-        )
-        for r in range(4):
-            nc.gpsimd.dma_start(
-                out=w_scales[r:P:32, :].rearrange("q (a n) -> q a n", a=PASSES).bitcast(I32),
-                in_=w4_scales.rearrange("a (q r) n -> r q a n", r=4)[r].bitcast(I32),
-            )
-            nc.scalar.dma_start(
-                out=x_scales[r:P:32, :].rearrange("q (a t) -> q a t", a=PASSES).bitcast(I32),
-                in_=x4_scales.rearrange("a (q r) t -> r q a t", r=4)[r].bitcast(I32),
-            )
         raw = {}
+
+        def load_words(tile, rows):
+            nc.sync.dma_start(
+                out=tile[:].rearrange("p (a c) -> p a c", a=PASSES).bitcast(I32),
+                in_=rows.rearrange("a p c -> p a c").bitcast(I32),
+            )
+
+        def load_scales(queue, tile, rows, r):
+            queue.dma_start(
+                out=tile[r:P:32, :].rearrange("q (a c) -> q a c", a=PASSES).bitcast(I32),
+                in_=rows.rearrange("a (q r) c -> r q a c", r=4)[r].bitcast(I32),
+            )
+
+        def load_xr(a, c):
+            raw[a, c] = keep.tile([P, PACK, CHUNK], F32, name=f"raw{a}{c}")
+            nc.sync.dma_start(
+                out=raw[a, c][:],
+                in_=xr[a * K_PASS : (a + 1) * K_PASS, c * CHUNK : (c + 1) * CHUNK].rearrange("(p j) t -> p j t", j=PACK),
+            )
+
+        load_words(w_words, w4_words)
+        for r in range(4):
+            load_scales(nc.scalar, w_scales, w4_scales, r)
+        for r in range(2):
+            load_scales(nc.sync, x_scales, x4_scales, r)
+        load_words(x_words, x4_words)
+        for r in range(2, 4):
+            load_scales(nc.sync, x_scales, x4_scales, r)
         for a in range(PASSES):
             for c in range(T // CHUNK):
-                raw[a, c] = keep.tile([P, PACK, CHUNK], F32, name=f"raw{a}{c}")
-                nc.sync.dma_start(
-                    out=raw[a, c][:],
-                    in_=xr[a * K_PASS : (a + 1) * K_PASS, c * CHUNK : (c + 1) * CHUNK].rearrange("(p j) t -> p j t", j=PACK),
-                )
+                load_xr(a, c)
 
         grouped, codes, scales, acc = {}, {}, {}, {}
 

@@ -17,7 +17,7 @@ P = 128
 PACK = 4
 K_PASS = P * PACK
 PASSES = K // K_PASS
-CHUNK = 768
+CHUNKS = (1024, 512)
 GROUP = 256
 TILES = T // P
 BANKS = 8
@@ -54,10 +54,11 @@ def tile_mix_xres_tm_none_kernel(tc, x4_words, x4_scales, xr, w4_words, w4_scale
             )
 
         def load_xr(a, c):
-            raw[a, c] = keep.tile([P, PACK, CHUNK], F32, name=f"raw{a}{c}")
+            first = sum(CHUNKS[:c])
+            raw[a, c] = keep.tile([P, PACK, CHUNKS[c]], F32, name=f"raw{a}{c}")
             nc.sync.dma_start(
                 out=raw[a, c][:],
-                in_=xr[a * K_PASS : (a + 1) * K_PASS, c * CHUNK : (c + 1) * CHUNK].rearrange("(p j) t -> p j t", j=PACK),
+                in_=xr[a * K_PASS : (a + 1) * K_PASS, first : first + CHUNKS[c]].rearrange("(p j) t -> p j t", j=PACK),
             )
 
         load_words(w_words, w4_words)
@@ -68,15 +69,15 @@ def tile_mix_xres_tm_none_kernel(tc, x4_words, x4_scales, xr, w4_words, w4_scale
         load_words(x_words, x4_words)
         for r in range(2, 4):
             load_scales(nc.sync, x_scales, x4_scales, r)
-        for a in range(PASSES):
-            for c in range(T // CHUNK):
+        for c in range(len(CHUNKS)):
+            for a in range(PASSES):
                 load_xr(a, c)
 
         grouped, codes, scales, acc = {}, {}, {}, {}
 
         def cast(copy, a, g):
             grouped[a, g] = keep.tile([P, GROUP, PACK], BF16, name=f"grouped{a}{g}", align_bytes=64)
-            c, first = divmod(g * GROUP, CHUNK)
+            c, first = divmod(g * GROUP, CHUNKS[0])
             copy(
                 out=grouped[a, g][:].rearrange("p (b i) j -> p b j i", i=4),
                 in_=raw[a, c][:, :, first : first + GROUP].rearrange("p j (b i) -> p b j i", i=4),
@@ -122,42 +123,30 @@ def tile_mix_xres_tm_none_kernel(tc, x4_words, x4_scales, xr, w4_words, w4_scale
 
         for i in range(BANKS):
             multiply_x4(i)
-        for first in (0, 3):
-            cast(act, 0, first + 2)
-            cast(vec, 0, first)
-            cast(vec, 0, first + 1)
-            for g in range(first, first + 3):
-                quantize(0, g)
-                if g < BANKS // 2:
-                    multiply_xr(0, g)
 
-        cast(act, 1, 2)
-        cast(vec, 1, 0)
-        cast(vec, 1, 1)
-        for g in range(3):
-            quantize(1, g)
-        multiply_xr(1, 0)
-        finish(act, 0)
-        finish(vec, 1)
-        multiply_xr(1, 1)
-        finish(act, 2)
-        finish(vec, 3)
-        for i in (8, 9):
-            multiply_x4(i)
-        multiply_xr(0, 4)
-        multiply_xr(1, 2)
-        finish(act, 4)
-        finish(act, 5)
-        for i in (10, 11):
-            multiply_x4(i)
-        multiply_xr(0, 5)
+        for a in range(PASSES):
+            cast(act, a, 3)
+            cast(vec, a, 0)
+            cast(vec, a, 1)
+            quantize(a, 0)
+            cast(vec, a, 2)
+            for g in (1, 2, 3):
+                quantize(a, g)
+            for g in range(4):
+                multiply_xr(a, g)
 
-        cast(act, 1, 5)
-        cast(vec, 1, 3)
-        cast(vec, 1, 4)
-        for g in range(3, 6):
-            quantize(1, g)
-        for g in range(3, 6):
-            multiply_xr(1, g)
+        for i in range(BANKS):
+            finish(act, i)
+        for a in range(PASSES):
+            for g in (4, 5):
+                cast(vec, a, g)
+            for g in (4, 5):
+                quantize(a, g)
+        for i in range(BANKS, TILES):
+            multiply_x4(i)
+        for a in range(PASSES):
+            for g in (4, 5):
+                multiply_xr(a, g)
+        for g in (4, 5):
             finish(act, 2 * g)
             finish(vec, 2 * g + 1)

@@ -17,7 +17,7 @@ P = 128
 PACK = 4
 K_PASS = P * PACK
 PASSES = K // K_PASS
-CHUNKS = (1024, 512)
+LOADS = ((0, 0, 768), (1, 0, 768), (0, 768, 1536), (1, 768, 1280), (1, 1280, 1536))
 GROUP = 256
 TILES = T // P
 BANKS = 8
@@ -53,13 +53,14 @@ def tile_mix_xres_tm_none_kernel(tc, x4_words, x4_scales, xr, w4_words, w4_scale
                 in_=rows.rearrange("a (q r) c -> r q a c", r=4)[r].bitcast(I32),
             )
 
-        def load_xr(a, c):
-            first = sum(CHUNKS[:c])
-            raw[a, c] = keep.tile([P, PACK, CHUNKS[c]], F32, name=f"raw{a}{c}")
+        def load_xr(a, first, end):
+            chunk = keep.tile([P, PACK, end - first], F32, name=f"raw{a}_{first}")
             nc.sync.dma_start(
-                out=raw[a, c][:],
-                in_=xr[a * K_PASS : (a + 1) * K_PASS, first : first + CHUNKS[c]].rearrange("(p j) t -> p j t", j=PACK),
+                out=chunk[:],
+                in_=xr[a * K_PASS : (a + 1) * K_PASS, first:end].rearrange("(p j) t -> p j t", j=PACK),
             )
+            for g in range(first // GROUP, end // GROUP):
+                raw[a, g] = chunk[:, :, g * GROUP - first : (g + 1) * GROUP - first]
 
         load_words(w_words, w4_words)
         for r in range(4):
@@ -69,19 +70,22 @@ def tile_mix_xres_tm_none_kernel(tc, x4_words, x4_scales, xr, w4_words, w4_scale
         load_words(x_words, x4_words)
         for r in range(2, 4):
             load_scales(nc.sync, x_scales, x4_scales, r)
-        for c in range(len(CHUNKS)):
-            for a in range(PASSES):
-                load_xr(a, c)
+        for load in LOADS:
+            load_xr(*load)
 
         grouped, codes, scales, acc = {}, {}, {}, {}
 
-        def cast(copy, a, g):
-            grouped[a, g] = keep.tile([P, GROUP, PACK], BF16, name=f"grouped{a}{g}", align_bytes=64)
-            c, first = divmod(g * GROUP, CHUNKS[0])
+        def cast(copy, a, g, first=0, end=GROUP):
+            if (a, g) not in grouped:
+                grouped[a, g] = keep.tile([P, GROUP, PACK], BF16, name=f"grouped{a}{g}", align_bytes=64)
             copy(
-                out=grouped[a, g][:].rearrange("p (b i) j -> p b j i", i=4),
-                in_=raw[a, c][:, :, first : first + GROUP].rearrange("p j (b i) -> p b j i", i=4),
+                out=grouped[a, g][:, first:end, :].rearrange("p (b i) j -> p b j i", i=4),
+                in_=raw[a, g][:, :, first:end].rearrange("p j (b i) -> p b j i", i=4),
             )
+
+        def share(a, g):
+            cast(vec, a, g, 0, P)
+            cast(act, a, g, P, GROUP)
 
         def quantize(a, g):
             codes[a, g] = keep.tile([P, GROUP], U32, name=f"codes{a}{g}", align_bytes=64)
@@ -124,29 +128,46 @@ def tile_mix_xres_tm_none_kernel(tc, x4_words, x4_scales, xr, w4_words, w4_scale
         for i in range(BANKS):
             multiply_x4(i)
 
-        for a in range(PASSES):
-            cast(act, a, 3)
-            cast(vec, a, 0)
-            cast(vec, a, 1)
-            quantize(a, 0)
-            cast(vec, a, 2)
-            for g in (1, 2, 3):
-                quantize(a, g)
-            for g in range(4):
-                multiply_xr(a, g)
+        cast(vec, 0, 0)
+        cast(vec, 0, 1)
+        quantize(0, 0)
+        share(0, 2)
+        quantize(0, 1)
+        quantize(0, 2)
+        for g in range(3):
+            multiply_xr(0, g)
 
-        for i in range(BANKS):
-            finish(act, i)
-        for a in range(PASSES):
-            for g in (4, 5):
-                cast(vec, a, g)
-            for g in (4, 5):
-                quantize(a, g)
+        for g in range(3):
+            share(1, g)
+        for g in range(3):
+            quantize(1, g)
+        for g in range(3):
+            multiply_xr(1, g)
+        finish(act, 0)
+        finish(vec, 1)
+        finish(act, 2)
+        finish(act, 3)
+
+        cast(vec, 0, 3)
+        share(0, 4)
+        quantize(0, 3)
+        share(0, 5)
+        quantize(0, 4)
+        quantize(0, 5)
+        finish(act, 4)
+        finish(act, 5)
         for i in range(BANKS, TILES):
             multiply_x4(i)
-        for a in range(PASSES):
-            for g in (4, 5):
-                multiply_xr(a, g)
-        for g in (4, 5):
-            finish(act, 2 * g)
-            finish(vec, 2 * g + 1)
+        for g in range(3, 6):
+            multiply_xr(0, g)
+
+        cast(vec, 1, 3)
+        share(1, 4)
+        quantize(1, 3)
+        quantize(1, 4)
+        share(1, 5)
+        quantize(1, 5)
+        for g in range(3, 6):
+            multiply_xr(1, g)
+        for i in range(6, TILES):
+            finish(vec if i in (8, 10) else act, i)

from contextlib import ExitStack

import concourse.mybir as mybir

K, N, T = 1024, 512, 1536
FLOPS = 2 * 2 * K * N * T

F32 = mybir.dt.float32
BF16 = mybir.dt.bfloat16
I32 = mybir.dt.int32
U32 = mybir.dt.uint32
U8 = mybir.dt.uint8
E4M3X4 = mybir.dt.float8_e4m3fn_x4
E2M1X4 = mybir.dt.float4_e2m1fn_x4

P = 128
PACK = 4
K_PASS = P * PACK
PASSES = K // K_PASS
LOADS = ((0, 0, 768), (1, 0, 768), (0, 768, 1536), (1, 768, 1280), (1, 1280, 1536))
GROUP = 256
TILES = T // P
BANKS = 8


def tile_mix_xres_tm_none_kernel(tc, x4_words, x4_scales, xr, w4_words, w4_scales, out):
    nc = tc.nc
    with ExitStack() as ctx:
        keep = ctx.enter_context(tc.tile_pool(name="keep", bufs=1))
        psum = ctx.enter_context(tc.psum_pool(name="psum", bufs=1))

        w_words = keep.tile([P, PASSES * 2 * N], U8, name="w_words", align_bytes=64)
        x_words = keep.tile([P, PASSES * 2 * T], U8, name="x_words", align_bytes=64)
        w_scales = keep.tile([P, PASSES * N], U8, name="w_scales", align_bytes=64)
        x_scales = keep.tile([P, PASSES * T], U8, name="x_scales", align_bytes=64)

        ctx.enter_context(tc.manual_schedule())

        nc.gpsimd.memset(w_scales[:].bitcast(I32), 0)
        nc.vector.memset(x_scales[:].bitcast(I32), 0)

        raw = {}

        def load_words(tile, rows):
            nc.sync.dma_start(
                out=tile[:].rearrange("p (a c) -> p a c", a=PASSES).bitcast(I32),
                in_=rows.rearrange("a p c -> p a c").bitcast(I32),
            )

        def load_scales(queue, tile, rows, r):
            queue.dma_start(
                out=tile[r:P:32, :].rearrange("q (a c) -> q a c", a=PASSES).bitcast(I32),
                in_=rows.rearrange("a (q r) c -> r q a c", r=4)[r].bitcast(I32),
            )

        def load_xr(a, first, end):
            chunk = keep.tile([P, PACK, end - first], F32, name=f"raw{a}_{first}")
            nc.sync.dma_start(
                out=chunk[:],
                in_=xr[a * K_PASS : (a + 1) * K_PASS, first:end].rearrange("(p j) t -> p j t", j=PACK),
            )
            for g in range(first // GROUP, end // GROUP):
                raw[a, g] = chunk[:, :, g * GROUP - first : (g + 1) * GROUP - first]

        load_words(w_words, w4_words)
        for r in range(4):
            load_scales(nc.scalar, w_scales, w4_scales, r)
        for r in range(2):
            load_scales(nc.sync, x_scales, x4_scales, r)
        load_words(x_words, x4_words)
        for r in range(2, 4):
            load_scales(nc.sync, x_scales, x4_scales, r)
        for load in LOADS:
            load_xr(*load)

        grouped, codes, scales, acc = {}, {}, {}, {}

        def cast(copy, a, g, first=0, end=GROUP):
            if (a, g) not in grouped:
                grouped[a, g] = keep.tile([P, GROUP, PACK], BF16, name=f"grouped{a}{g}", align_bytes=64)
            copy(
                out=grouped[a, g][:, first:end, :].rearrange("p (b i) j -> p b j i", i=4),
                in_=raw[a, g][:, :, first:end].rearrange("p j (b i) -> p b j i", i=4),
            )

        def share(a, g):
            cast(vec, a, g, 0, P)
            cast(act, a, g, P, GROUP)

        def quantize(a, g):
            codes[a, g] = keep.tile([P, GROUP], U32, name=f"codes{a}{g}", align_bytes=64)
            scales[a, g] = keep.tile([P, GROUP], U8, name=f"scales{a}{g}", align_bytes=64)
            nc.vector.quantize_mx(
                out=codes[a, g][:].bitcast(E4M3X4),
                scales=scales[a, g][:],
                in_=grouped[a, g][:].rearrange("p t j -> p (t j)"),
            )

        def multiply(i, a, lhs, lhs_scale, start, stop):
            nc.tensor.matmul_mx(
                out=acc[i][:],
                lhsT=lhs,
                lhsT_scale=lhs_scale,
                rhs=w_words[:, a * 2 * N : (a + 1) * 2 * N].bitcast(E2M1X4),
                rhs_scale=w_scales[:, a * N : (a + 1) * N],
                start=start,
                stop=stop,
            )

        def multiply_x4(i):
            acc[i] = psum.tile([P, N], F32, name=f"acc{i % BANKS}")
            for a in range(PASSES):
                col = a * T + i * P
                multiply(i, a, x_words[:, 2 * col : 2 * (col + P)].bitcast(E2M1X4), x_scales[:, col : col + P], a == 0, False)

        def multiply_xr(a, g):
            for h in range(GROUP // P):
                cols = slice(h * P, (h + 1) * P)
                multiply(g * (GROUP // P) + h, a, codes[a, g][:, cols].bitcast(E4M3X4), scales[a, g][:, cols], False, a == PASSES - 1)

        def finish(copy, i):
            result = keep.tile([P, N], F32, name=f"result{i}")
            copy(out=result[:], in_=acc[i][:])
            nc.sync.dma_start(out=out[i * P : (i + 1) * P, :], in_=result[:])

        vec, act = nc.vector.tensor_copy, nc.scalar.copy

        for i in range(BANKS):
            multiply_x4(i)

        cast(vec, 0, 0)
        cast(vec, 0, 1)
        quantize(0, 0)
        share(0, 2)
        quantize(0, 1)
        quantize(0, 2)
        for g in range(3):
            multiply_xr(0, g)

        for g in range(3):
            share(1, g)
        for g in range(3):
            quantize(1, g)
        for g in range(3):
            multiply_xr(1, g)
        finish(act, 0)
        finish(vec, 1)
        finish(act, 2)
        finish(act, 3)

        cast(vec, 0, 3)
        share(0, 4)
        quantize(0, 3)
        share(0, 5)
        quantize(0, 4)
        quantize(0, 5)
        finish(act, 4)
        finish(act, 5)
        for i in range(BANKS, TILES):
            multiply_x4(i)
        for g in range(3, 6):
            multiply_xr(0, g)

        cast(vec, 1, 3)
        share(1, 4)
        quantize(1, 3)
        quantize(1, 4)
        share(1, 5)
        quantize(1, 5)
        for g in range(3, 6):
            multiply_xr(1, g)
        for i in range(6, TILES):
            finish(vec if i in (8, 10) else act, i)
